import numpy as np
import ml_dtypes


def mxq(x, axis, fmt="e4m3"):
    dtype, down = {"e4m3": (ml_dtypes.float8_e4m3fn, 7), "e5m2": (ml_dtypes.float8_e5m2, 14)}[fmt]
    v = np.moveaxis(np.asarray(x, np.float32).astype(ml_dtypes.bfloat16).astype(np.float64), axis, -1)
    blocks = v.reshape(v.shape[:-1] + (-1, 32))
    amax = np.abs(blocks).max(-1, keepdims=True)
    byte = np.maximum(np.where(amax > 0, np.frexp(amax)[1] - 1 + 127, 0) - down, 1)
    scale = np.exp2(byte - 127.0)
    codes = (blocks / scale).astype(np.float32).astype(dtype).astype(np.float64)
    return np.moveaxis((codes * scale).reshape(v.shape), -1, axis)


WIDE = False


def mx_kscale(k):
    if not WIDE:
        return np.ones(k)
    levels = np.array([10, -10, 5, -5, 0])
    if k % 512:
        return np.exp2(np.random.permutation(np.resize(levels, k // 32))).repeat(32)
    a = np.empty((k // 512, 16))
    for p in range(k // 512):
        a[p, :8] = np.random.permutation(np.resize(levels, 8))
        for g in range(8):
            far = levels[np.abs(levels - a[p, g]) >= 10]
            a[p, g + 8] = far[np.random.randint(len(far))]
    return np.exp2(a.ravel()).repeat(32)


def f64(x):
    return np.asarray(x).astype(np.float64)


def striped(idx):
    return np.tile(idx.reshape(-1, 16).T, (8, 1)).astype(np.uint16)


def unstriped(offs):
    return offs[:16].T.reshape(-1).astype(np.int64)


E2M1 = np.array([0.0, 0.5, 1.0, 1.5, 2.0, 3.0, 4.0, 6.0, -0.0, -0.5, -1.0, -1.5, -2.0, -3.0, -4.0, -6.0])


def pack_weight(w, fmt):
    k, n = w.shape
    w = f64(np.asarray(w, np.float32).astype(ml_dtypes.bfloat16)).reshape(k // 32, 32, n)
    amax = np.abs(w).max(1)
    if fmt == "e4m3":
        byte = np.frexp(amax)[1] - 1 + 127 - 7
    else:
        mant, ex = np.frexp(amax / 6.0)
        byte = np.where(mant > 0.5, ex, ex - 1) + 127
    byte = np.clip(np.where(amax > 0, byte, 1), 1, 254)
    scaled = (w * np.exp2(127.0 - byte)[:, None, :]).reshape(k, n).astype(np.float32)
    by_word = np.ascontiguousarray(scaled.reshape(k // 512, 128, 4, n).transpose(0, 1, 3, 2))
    if fmt == "e4m3":
        words = by_word.astype(ml_dtypes.float8_e4m3fn).view(np.uint8)
    else:
        c = by_word.astype(ml_dtypes.float4_e2m1fn).view(np.uint8) & 0xF
        words = (c[..., 0::2] | (c[..., 1::2] << 4)).reshape(k // 512, 128, 2 * n)
    return np.ascontiguousarray(words), np.ascontiguousarray(byte.astype(np.uint8).reshape(k // 512, 16, n))


def unpack_weight(words, scales, fmt):
    g, _, n = scales.shape
    words = np.ascontiguousarray(words).reshape(g, 128, n, -1)
    if fmt == "e4m3":
        vals = words.view(ml_dtypes.float8_e4m3fn).astype(np.float64)
    else:
        nib = np.empty((g, 128, n, 4), np.uint8)
        nib[..., 0::2] = words & 0xF
        nib[..., 1::2] = words >> 4
        vals = E2M1[nib]
    vals = vals * np.repeat(np.exp2(scales.astype(np.float64) - 127.0), 8, axis=1)[..., None]
    return vals.transpose(0, 1, 3, 2).reshape(g * 512, n)


def silu(v):
    return v / (1.0 + np.exp(-np.maximum(v, -700.0)))


K, T, E, C, H, N = 512, 1024, 6, 128, 512, 128


def by_expert(wq, xq):
    return np.concatenate([wq[e].T @ xq[:, e * C:(e + 1) * C] for e in range(E)], axis=1)


def setup_inputs():
    n = np.random.standard_normal
    s = mx_kscale(K)[:, None]
    u = mx_kscale(H)
    w1 = [pack_weight(m, "e2m1") for m in n((E + 1, K, H)) / np.sqrt(K) / s[None]]
    w3 = [pack_weight(m, "e2m1") for m in n((E + 1, K, H)) / np.sqrt(K) / s[None] * u[None, None, :]]
    w2 = [pack_weight(m, "e2m1") for m in n((E + 1, H, N)) / np.sqrt(H) / u[None, :, None]]
    return {
        "xT": (n((K, T)) * s).astype(np.float32),
        "w1_words": np.stack([m[0] for m in w1]),
        "w1_scales": np.stack([m[1] for m in w1]),
        "w3_words": np.stack([m[0] for m in w3]),
        "w3_scales": np.stack([m[1] for m in w3]),
        "w2_words": np.stack([m[0] for m in w2]),
        "w2_scales": np.stack([m[1] for m in w2]),
        "gate": np.tile(np.random.uniform(0.2, 1.0, E * C), (N, 1)).astype(np.float32),
        "offs": striped(np.random.permutation(T)[:E * C]),
    }


def reference(xT, w1_words, w1_scales, w3_words, w3_scales, w2_words, w2_scales, gate, offs):
    idx = unstriped(offs)
    w1 = np.stack([unpack_weight(w1_words[e], w1_scales[e], "e2m1") for e in range(E + 1)])
    w3 = np.stack([unpack_weight(w3_words[e], w3_scales[e], "e2m1") for e in range(E + 1)])
    w2 = np.stack([unpack_weight(w2_words[e], w2_scales[e], "e2m1") for e in range(E + 1)])
    w1q, w3q, w2q = w1, w3, w2
    xs = mxq(f64(xT), 0, "e4m3")
    hs = silu(w1q[E].T @ xs) * (w3q[E].T @ xs)
    ys = w2q[E].T @ mxq(hs, 0, "e4m3")
    xq = mxq(f64(xT)[:, idx], 0, "e4m3")
    h = silu(by_expert(w1q, xq))
    h = h * by_expert(w3q, xq)
    y = by_expert(w2q, mxq(h, 0, "e4m3"))
    out = ys
    out[:, idx] += f64(gate) * y
    return out

@@ -1,0 +1,199 @@
+from contextlib import ExitStack
+
+import concourse.mybir as mybir
+from concourse.masks import make_identity
+
+F32 = mybir.dt.float32
+BF16 = mybir.dt.bfloat16
+I32 = mybir.dt.int32
+U32 = mybir.dt.uint32
+U16 = mybir.dt.uint16
+U8 = mybir.dt.uint8
+FP8X4 = mybir.dt.float8_e4m3fn_x4
+FP4X4 = mybir.dt.float4_e2m1fn_x4
+SILU = mybir.ActivationFunctionType.Silu
+MULT = mybir.AluOpType.mult
+ADD = mybir.AluOpType.add
+
+P = 128
+K, T, E, C, H, N = 512, 1024, 6, 128, 512, 128
+SHARED = E
+UNIT = 256
+TILES = UNIT // P
+FLOPS = 2 * (E * C + T) * (2 * K * H + H * N)
+
+
+def tile_moe_shr_glu_silu_kernel(tc, xT, w1_words, w1_scales, w3_words, w3_scales, w2_words, w2_scales, gate, offs, out):
+    nc = tc.nc
+    with ExitStack() as ctx:
+        keep = ctx.enter_context(tc.tile_pool(name="keep", bufs=1))
+        work = ctx.enter_context(tc.tile_pool(name="work", bufs=3))
+        psum = ctx.enter_context(tc.psum_pool(name="psum", bufs=2))
+
+        offsets = keep.tile([P, E * C // 16], U16, name="offsets")
+        raw = [keep.tile([P, 4, UNIT], F32, name=f"raw{c}") for c in range(4)]
+        pairs = keep.tile([P, 2, 2 * T], BF16, name="pairs", align_bytes=64)
+        w1 = keep.tile([P, E + 1, 2 * H], U8, name="w1", align_bytes=64)
+        w3 = keep.tile([P, E + 1, 2 * H], U8, name="w3", align_bytes=64)
+        w2 = keep.tile([P, E + 1, 2 * N], U8, name="w2", align_bytes=64)
+        s1 = keep.tile([P, E + 1, H], U8, name="s1", align_bytes=64)
+        s3 = keep.tile([P, E + 1, H], U8, name="s3", align_bytes=64)
+        s2 = keep.tile([P, E + 1, N], U8, name="s2", align_bytes=64)
+        gates = keep.tile([P, E * C], F32, name="gates")
+        scattered = keep.tile([P, T], F32, name="scattered")
+        result = keep.tile([P, T], F32, name="result")
+        early = keep.tile([P, 2 * UNIT], F32, name="early")
+        ident = keep.tile([P, P], F32, name="ident")
+        warm = keep.tile([P, 1], F32, name="warm")
+
+        def zero(eng, t):
+            eng.memset(t[:].rearrange("p e n -> p (e n)").bitcast(I32), 0)
+
+        nc.vector.memset(warm[:], 0.0)
+        nc.scalar.activation(warm[:], warm[:], SILU)
+        zero(nc.vector, s1)
+        zero(nc.vector, s3)
+        zero(nc.vector, s2)
+        make_identity(nc, ident[:])
+        nc.gpsimd.memset(scattered[:], 0.0)
+
+        def load_x(c):
+            nc.sync.dma_start(out=raw[c][:], in_=xT.rearrange("(p j) t -> p j t", j=4)[:, :, c * UNIT : (c + 1) * UNIT])
+
+        def load_words(tile, words, a, b):
+            nc.sync.dma_start(
+                out=tile[:, a:b, :].bitcast(I32),
+                in_=words[a:b, 0].bitcast(I32).rearrange("e p n -> p e n"),
+            )
+
+        def load_scales(eng, tile, scales):
+            view = scales.bitcast(I32).rearrange("e s (q r) n -> r q (e s) n", r=4)
+            for r in range(4):
+                eng.dma_start(out=tile[r:P:32, :, :].bitcast(I32), in_=view[r])
+
+        load_x(0)
+        load_words(w1, w1_words, SHARED, SHARED + 1)
+        load_words(w3, w3_words, SHARED, SHARED + 1)
+        load_scales(nc.scalar, s1, w1_scales)
+        load_scales(nc.gpsimd, s3, w3_scales)
+        load_x(1)
+        load_x(2)
+        nc.sync.dma_start(offsets[:], offs)
+        load_x(3)
+        load_words(w2, w2_words, 0, E + 1)
+        load_scales(nc.gpsimd, s2, w2_scales)
+        for a in (0, 2, 4):
+            load_words(w1, w1_words, a, a + 2)
+            load_words(w3, w3_words, a, a + 2)
+            if a == 0:
+                nc.sync.dma_start(out=gates[:], in_=gate)
+
+        def interleave(c, copy):
+            quads = work.tile([P, UNIT, 4], BF16, name="quads", align_bytes=64)
+            copy(quads[:].rearrange("p (c i) j -> p c j i", i=4), raw[c][:].rearrange("p j (c i) -> p c j i", i=4))
+            return quads[:].rearrange("p c j -> p (c j)")
+
+        def make_pairs(c):
+            nc.vector.tensor_copy(
+                pairs[:, :, c * 2 * UNIT : (c + 1) * 2 * UNIT].rearrange("p h (t e) -> p h t e", e=2),
+                raw[c][:].rearrange("p (h e) t -> p h t e", e=2),
+            )
+
+        def gather(u):
+            quads = work.tile([P, UNIT, 4], BF16, name="quads", align_bytes=64)
+            flat = quads[:].rearrange("p c j -> p (c j)")
+            words = flat.bitcast(U32).rearrange("p (c h) -> p c h", h=2)
+            for h in range(2):
+                nc.vector.tensor_copy(
+                    words[:, :, h],
+                    pairs[:, h, :].bitcast(U32).indirect(offsets[:, u * UNIT // 16 : (u + 1) * UNIT // 16]),
+                )
+            return flat
+
+        def quantize(tag, flat):
+            codes = work.tile([P, UNIT], U32, name=tag + "_codes", align_bytes=64)
+            scales = work.tile([P, UNIT], U8, name=tag + "_scales", align_bytes=64)
+            nc.vector.quantize_mx(out=codes[:].bitcast(FP8X4), scales=scales[:], in_=flat)
+            return codes, scales
+
+        def hidden(codes, scales, experts):
+            back = psum.tile([P, TILES, 2, P], F32, name="back")
+            for t, e in enumerate(experts):
+                cols = slice(t * P, (t + 1) * P)
+                a = psum.tile([P, H], F32, name="a")
+                b = psum.tile([P, H], F32, name="b")
+                for acc, w, s in ((a, w1, s1), (b, w3, s3)):
+                    nc.tensor.matmul_mx(
+                        out=acc[:], lhsT=codes[:, cols].bitcast(FP8X4), lhsT_scale=scales[:, cols],
+                        rhs=w[:, e, :].bitcast(FP4X4), rhs_scale=s[:, e, :], start=True, stop=True,
+                    )
+                act = work.tile([P, H], F32, name="act")
+                nc.scalar.activation(
+                    act[:].rearrange("p (u m e) -> p u m e", u=2, e=2),
+                    a[:].rearrange("p (m u e) -> p u m e", u=2, e=2),
+                    SILU,
+                )
+                h = work.tile([P, H], BF16, name="h")
+                nc.vector.tensor_tensor(
+                    h[:].rearrange("p (u m e) -> p u m e", u=2, e=2),
+                    act[:].rearrange("p (u m e) -> p u m e", u=2, e=2),
+                    b[:].rearrange("p (m u e) -> p u m e", u=2, e=2),
+                    MULT,
+                )
+                hw = h[:].bitcast(F32)
+                for u in range(2):
+                    nc.tensor.transpose(back[:, t, u, :], hw[:, u * P : (u + 1) * P], ident[:])
+            turned = work.tile([P, UNIT, 4], BF16, name="turned", align_bytes=64)
+            flat = turned[:].rearrange("p c j -> p (c j)")
+            nc.scalar.copy(
+                flat.bitcast(F32).rearrange("p (t r u) -> p t r u", t=TILES, u=2),
+                back[:].rearrange("p t u r -> p t r u"),
+            )
+            return quantize("h", flat)
+
+        def last(y, codes, scales, experts):
+            for t, e in enumerate(experts):
+                cols = slice(t * P, (t + 1) * P)
+                nc.tensor.matmul_mx(
+                    out=y[:, cols], lhsT=w2[:, e, :].bitcast(FP4X4), lhsT_scale=s2[:, e, :],
+                    rhs=codes[:, cols].bitcast(FP8X4), rhs_scale=scales[:, cols], start=True, stop=True,
+                )
+
+        def shared_unit(c, copy):
+            flat = interleave(c, copy)
+            codes, scales = quantize("x", flat)
+            hc, hs = hidden(codes, scales, (SHARED,) * TILES)
+            y = psum.tile([P, UNIT], F32, name="y")
+            last(y, hc, hs, (SHARED,) * TILES)
+            return y
+
+        def routed_unit(u):
+            flat = gather(u)
+            codes, scales = quantize("x", flat)
+            experts = tuple(range(u * TILES, (u + 1) * TILES))
+            hc, hs = hidden(codes, scales, experts)
+            y = psum.tile([P, UNIT], F32, name="y")
+            last(y, hc, hs, experts)
+            ysb = work.tile([P, UNIT], F32, name="ysb")
+            nc.scalar.copy(ysb[:], y[:])
+            nc.vector.tensor_tensor(
+                scattered[:].indirect(offsets[:, u * UNIT // 16 : (u + 1) * UNIT // 16]),
+                ysb[:], gates[:, u * UNIT : (u + 1) * UNIT], MULT,
+            )
+
+        y = shared_unit(0, nc.vector.tensor_copy)
+        nc.scalar.copy(early[:, 0:UNIT], y[:])
+        y = shared_unit(1, nc.scalar.copy)
+        nc.scalar.copy(early[:, UNIT : 2 * UNIT], y[:])
+        for c in range(4):
+            make_pairs(c)
+        for u in range(3):
+            routed_unit(u)
+        half = slice(0, 2 * UNIT)
+        nc.vector.tensor_tensor(result[:, half], early[:], scattered[:, half], ADD)
+        nc.sync.dma_start(out=out[:, half], in_=result[:, half])
+        for c in (2, 3):
+            y = shared_unit(c, nc.scalar.copy)
+            cols = slice(c * UNIT, (c + 1) * UNIT)
+            nc.vector.tensor_tensor(result[:, cols], y[:], scattered[:, cols], ADD)
+            nc.sync.dma_start(out=out[:, cols], in_=result[:, cols])

@@ -55,7 +55,6 @@ def tile_moe_shr_glu_silu_kernel(tc, xT, w1_words, w1_scales, w3_words, w3_scale
         zero(nc.vector, s3)
         zero(nc.vector, s2)
         make_identity(nc, ident[:])
-        nc.gpsimd.memset(scattered[:], 0.0)
 
         def load_x(c):
             nc.sync.dma_start(out=raw[c][:], in_=xT.rearrange("(p j) t -> p j t", j=4)[:, :, c * UNIT : (c + 1) * UNIT])
@@ -88,13 +87,15 @@ def tile_moe_shr_glu_silu_kernel(tc, xT, w1_words, w1_scales, w3_words, w3_scale
             if a == 0:
                 nc.sync.dma_start(out=gates[:], in_=gate)
 
+        nc.gpsimd.memset(scattered[:], 0.0)
+
         def interleave(c, copy):
             quads = work.tile([P, UNIT, 4], BF16, name="quads", align_bytes=64)
             copy(quads[:].rearrange("p (c i) j -> p c j i", i=4), raw[c][:].rearrange("p j (c i) -> p c j i", i=4))
             return quads[:].rearrange("p c j -> p (c j)")
 
-        def make_pairs(c):
-            nc.vector.tensor_copy(
+        def make_pairs(c, copy):
+            copy(
                 pairs[:, :, c * 2 * UNIT : (c + 1) * 2 * UNIT].rearrange("p h (t e) -> p h t e", e=2),
                 raw[c][:].rearrange("p (h e) t -> p h t e", e=2),
             )
@@ -111,13 +112,20 @@ def tile_moe_shr_glu_silu_kernel(tc, xT, w1_words, w1_scales, w3_words, w3_scale
             return flat
 
         def quantize(tag, flat):
-            codes = work.tile([P, UNIT], U32, name=tag + "_codes", align_bytes=64)
-            scales = work.tile([P, UNIT], U8, name=tag + "_scales", align_bytes=64)
+            width = flat.shape[1] // 4
+            codes = work.tile([P, width], U32, name=tag + "_codes", align_bytes=64)
+            scales = work.tile([P, width], U8, name=tag + "_scales", align_bytes=64)
             nc.vector.quantize_mx(out=codes[:].bitcast(FP8X4), scales=scales[:], in_=flat)
             return codes, scales
 
+        def finish(y, at):
+            cols = slice(at, at + y.shape[1])
+            nc.vector.tensor_tensor(result[:, cols], y[:], scattered[:, cols], ADD)
+            nc.sync.dma_start(out=out[:, cols], in_=result[:, cols])
+
         def hidden(codes, scales, experts):
-            back = psum.tile([P, TILES, 2, P], F32, name="back")
+            tiles = len(experts)
+            back = psum.tile([P, tiles, 2, P], F32, name="back")
             for t, e in enumerate(experts):
                 cols = slice(t * P, (t + 1) * P)
                 a = psum.tile([P, H], F32, name="a")
@@ -143,10 +151,10 @@ def tile_moe_shr_glu_silu_kernel(tc, xT, w1_words, w1_scales, w3_words, w3_scale
                 hw = h[:].bitcast(F32)
                 for u in range(2):
                     nc.tensor.transpose(back[:, t, u, :], hw[:, u * P : (u + 1) * P], ident[:])
-            turned = work.tile([P, UNIT, 4], BF16, name="turned", align_bytes=64)
+            turned = work.tile([P, tiles * P, 4], BF16, name="turned", align_bytes=64)
             flat = turned[:].rearrange("p c j -> p (c j)")
             nc.scalar.copy(
-                flat.bitcast(F32).rearrange("p (t r u) -> p t r u", t=TILES, u=2),
+                flat.bitcast(F32).rearrange("p (t r u) -> p t r u", t=tiles, u=2),
                 back[:].rearrange("p t u r -> p t r u"),
             )
             return quantize("h", flat)
@@ -186,14 +194,18 @@ def tile_moe_shr_glu_silu_kernel(tc, xT, w1_words, w1_scales, w3_words, w3_scale
         y = shared_unit(1, nc.scalar.copy)
         nc.scalar.copy(early[:, UNIT : 2 * UNIT], y[:])
         for c in range(4):
-            make_pairs(c)
+            make_pairs(c, nc.vector.tensor_copy)
         for u in range(3):
             routed_unit(u)
         half = slice(0, 2 * UNIT)
         nc.vector.tensor_tensor(result[:, half], early[:], scattered[:, half], ADD)
         nc.sync.dma_start(out=out[:, half], in_=result[:, half])
-        for c in (2, 3):
-            y = shared_unit(c, nc.scalar.copy)
-            cols = slice(c * UNIT, (c + 1) * UNIT)
-            nc.vector.tensor_tensor(result[:, cols], y[:], scattered[:, cols], ADD)
-            nc.sync.dma_start(out=out[:, cols], in_=result[:, cols])
+        y = shared_unit(2, nc.scalar.copy)
+        finish(y, 2 * UNIT)
+        codes, scales = quantize("x", interleave(3, nc.scalar.copy))
+        for t in range(TILES):
+            cols = slice(t * P, (t + 1) * P)
+            hc, hs = hidden(codes[:, cols], scales[:, cols], (SHARED,))
+            y = psum.tile([P, P], F32, name="y")
+            last(y, hc, hs, (SHARED,))
+            finish(y, 3 * UNIT + t * P)

from contextlib import ExitStack

import concourse.mybir as mybir
from concourse.masks import make_identity

F32 = mybir.dt.float32
BF16 = mybir.dt.bfloat16
I32 = mybir.dt.int32
U32 = mybir.dt.uint32
U16 = mybir.dt.uint16
U8 = mybir.dt.uint8
FP8X4 = mybir.dt.float8_e4m3fn_x4
FP4X4 = mybir.dt.float4_e2m1fn_x4
SILU = mybir.ActivationFunctionType.Silu
MULT = mybir.AluOpType.mult
ADD = mybir.AluOpType.add

P = 128
K, T, E, C, H, N = 512, 1024, 6, 128, 512, 128
SHARED = E
UNIT = 256
TILES = UNIT // P
FLOPS = 2 * (E * C + T) * (2 * K * H + H * N)


def tile_moe_shr_glu_silu_kernel(tc, xT, w1_words, w1_scales, w3_words, w3_scales, w2_words, w2_scales, gate, offs, out):
    nc = tc.nc
    with ExitStack() as ctx:
        keep = ctx.enter_context(tc.tile_pool(name="keep", bufs=1))
        work = ctx.enter_context(tc.tile_pool(name="work", bufs=3))
        psum = ctx.enter_context(tc.psum_pool(name="psum", bufs=2))

        offsets = keep.tile([P, E * C // 16], U16, name="offsets")
        raw = [keep.tile([P, 4, UNIT], F32, name=f"raw{c}") for c in range(4)]
        pairs = keep.tile([P, 2, 2 * T], BF16, name="pairs", align_bytes=64)
        w1 = keep.tile([P, E + 1, 2 * H], U8, name="w1", align_bytes=64)
        w3 = keep.tile([P, E + 1, 2 * H], U8, name="w3", align_bytes=64)
        w2 = keep.tile([P, E + 1, 2 * N], U8, name="w2", align_bytes=64)
        s1 = keep.tile([P, E + 1, H], U8, name="s1", align_bytes=64)
        s3 = keep.tile([P, E + 1, H], U8, name="s3", align_bytes=64)
        s2 = keep.tile([P, E + 1, N], U8, name="s2", align_bytes=64)
        gates = keep.tile([P, E * C], F32, name="gates")
        scattered = keep.tile([P, T], F32, name="scattered")
        result = keep.tile([P, T], F32, name="result")
        early = keep.tile([P, 2 * UNIT], F32, name="early")
        ident = keep.tile([P, P], F32, name="ident")
        warm = keep.tile([P, 1], F32, name="warm")

        def zero(eng, t):
            eng.memset(t[:].rearrange("p e n -> p (e n)").bitcast(I32), 0)

        nc.vector.memset(warm[:], 0.0)
        nc.scalar.activation(warm[:], warm[:], SILU)
        zero(nc.vector, s1)
        zero(nc.vector, s3)
        zero(nc.vector, s2)
        make_identity(nc, ident[:])

        def load_x(c):
            nc.sync.dma_start(out=raw[c][:], in_=xT.rearrange("(p j) t -> p j t", j=4)[:, :, c * UNIT : (c + 1) * UNIT])

        def load_words(tile, words, a, b):
            nc.sync.dma_start(
                out=tile[:, a:b, :].bitcast(I32),
                in_=words[a:b, 0].bitcast(I32).rearrange("e p n -> p e n"),
            )

        def load_scales(eng, tile, scales):
            view = scales.bitcast(I32).rearrange("e s (q r) n -> r q (e s) n", r=4)
            for r in range(4):
                eng.dma_start(out=tile[r:P:32, :, :].bitcast(I32), in_=view[r])

        load_x(0)
        load_words(w1, w1_words, SHARED, SHARED + 1)
        load_words(w3, w3_words, SHARED, SHARED + 1)
        load_scales(nc.scalar, s1, w1_scales)
        load_scales(nc.gpsimd, s3, w3_scales)
        load_x(1)
        load_x(2)
        nc.sync.dma_start(offsets[:], offs)
        load_x(3)
        load_words(w2, w2_words, 0, E + 1)
        load_scales(nc.gpsimd, s2, w2_scales)
        for a in (0, 2, 4):
            load_words(w1, w1_words, a, a + 2)
            load_words(w3, w3_words, a, a + 2)
            if a == 0:
                nc.sync.dma_start(out=gates[:], in_=gate)

        nc.gpsimd.memset(scattered[:], 0.0)

        def interleave(c, copy):
            quads = work.tile([P, UNIT, 4], BF16, name="quads", align_bytes=64)
            copy(quads[:].rearrange("p (c i) j -> p c j i", i=4), raw[c][:].rearrange("p j (c i) -> p c j i", i=4))
            return quads[:].rearrange("p c j -> p (c j)")

        def make_pairs(c, copy):
            copy(
                pairs[:, :, c * 2 * UNIT : (c + 1) * 2 * UNIT].rearrange("p h (t e) -> p h t e", e=2),
                raw[c][:].rearrange("p (h e) t -> p h t e", e=2),
            )

        def gather(u):
            quads = work.tile([P, UNIT, 4], BF16, name="quads", align_bytes=64)
            flat = quads[:].rearrange("p c j -> p (c j)")
            words = flat.bitcast(U32).rearrange("p (c h) -> p c h", h=2)
            for h in range(2):
                nc.vector.tensor_copy(
                    words[:, :, h],
                    pairs[:, h, :].bitcast(U32).indirect(offsets[:, u * UNIT // 16 : (u + 1) * UNIT // 16]),
                )
            return flat

        def quantize(tag, flat):
            width = flat.shape[1] // 4
            codes = work.tile([P, width], U32, name=tag + "_codes", align_bytes=64)
            scales = work.tile([P, width], U8, name=tag + "_scales", align_bytes=64)
            nc.vector.quantize_mx(out=codes[:].bitcast(FP8X4), scales=scales[:], in_=flat)
            return codes, scales

        def finish(y, at):
            cols = slice(at, at + y.shape[1])
            nc.vector.tensor_tensor(result[:, cols], y[:], scattered[:, cols], ADD)
            nc.sync.dma_start(out=out[:, cols], in_=result[:, cols])

        def hidden(codes, scales, experts):
            tiles = len(experts)
            back = psum.tile([P, tiles, 2, P], F32, name="back")
            for t, e in enumerate(experts):
                cols = slice(t * P, (t + 1) * P)
                a = psum.tile([P, H], F32, name="a")
                b = psum.tile([P, H], F32, name="b")
                for acc, w, s in ((a, w1, s1), (b, w3, s3)):
                    nc.tensor.matmul_mx(
                        out=acc[:], lhsT=codes[:, cols].bitcast(FP8X4), lhsT_scale=scales[:, cols],
                        rhs=w[:, e, :].bitcast(FP4X4), rhs_scale=s[:, e, :], start=True, stop=True,
                    )
                act = work.tile([P, H], F32, name="act")
                nc.scalar.activation(
                    act[:].rearrange("p (u m e) -> p u m e", u=2, e=2),
                    a[:].rearrange("p (m u e) -> p u m e", u=2, e=2),
                    SILU,
                )
                h = work.tile([P, H], BF16, name="h")
                nc.vector.tensor_tensor(
                    h[:].rearrange("p (u m e) -> p u m e", u=2, e=2),
                    act[:].rearrange("p (u m e) -> p u m e", u=2, e=2),
                    b[:].rearrange("p (m u e) -> p u m e", u=2, e=2),
                    MULT,
                )
                hw = h[:].bitcast(F32)
                for u in range(2):
                    nc.tensor.transpose(back[:, t, u, :], hw[:, u * P : (u + 1) * P], ident[:])
            turned = work.tile([P, tiles * P, 4], BF16, name="turned", align_bytes=64)
            flat = turned[:].rearrange("p c j -> p (c j)")
            nc.scalar.copy(
                flat.bitcast(F32).rearrange("p (t r u) -> p t r u", t=tiles, u=2),
                back[:].rearrange("p t u r -> p t r u"),
            )
            return quantize("h", flat)

        def last(y, codes, scales, experts):
            for t, e in enumerate(experts):
                cols = slice(t * P, (t + 1) * P)
                nc.tensor.matmul_mx(
                    out=y[:, cols], lhsT=w2[:, e, :].bitcast(FP4X4), lhsT_scale=s2[:, e, :],
                    rhs=codes[:, cols].bitcast(FP8X4), rhs_scale=scales[:, cols], start=True, stop=True,
                )

        def shared_unit(c, copy):
            flat = interleave(c, copy)
            codes, scales = quantize("x", flat)
            hc, hs = hidden(codes, scales, (SHARED,) * TILES)
            y = psum.tile([P, UNIT], F32, name="y")
            last(y, hc, hs, (SHARED,) * TILES)
            return y

        def routed_unit(u):
            flat = gather(u)
            codes, scales = quantize("x", flat)
            experts = tuple(range(u * TILES, (u + 1) * TILES))
            hc, hs = hidden(codes, scales, experts)
            y = psum.tile([P, UNIT], F32, name="y")
            last(y, hc, hs, experts)
            ysb = work.tile([P, UNIT], F32, name="ysb")
            nc.scalar.copy(ysb[:], y[:])
            nc.vector.tensor_tensor(
                scattered[:].indirect(offsets[:, u * UNIT // 16 : (u + 1) * UNIT // 16]),
                ysb[:], gates[:, u * UNIT : (u + 1) * UNIT], MULT,
            )

        y = shared_unit(0, nc.vector.tensor_copy)
        nc.scalar.copy(early[:, 0:UNIT], y[:])
        y = shared_unit(1, nc.scalar.copy)
        nc.scalar.copy(early[:, UNIT : 2 * UNIT], y[:])
        for c in range(4):
            make_pairs(c, nc.vector.tensor_copy)
        for u in range(3):
            routed_unit(u)
        half = slice(0, 2 * UNIT)
        nc.vector.tensor_tensor(result[:, half], early[:], scattered[:, half], ADD)
        nc.sync.dma_start(out=out[:, half], in_=result[:, half])
        y = shared_unit(2, nc.scalar.copy)
        finish(y, 2 * UNIT)
        codes, scales = quantize("x", interleave(3, nc.scalar.copy))
        for t in range(TILES):
            cols = slice(t * P, (t + 1) * P)
            hc, hs = hidden(codes[:, cols], scales[:, cols], (SHARED,))
            y = psum.tile([P, P], F32, name="y")
            last(y, hc, hs, (SHARED,))
            finish(y, 3 * UNIT + t * P)
